import numpy as np
import ml_dtypes


def mxq(x, axis, fmt="e4m3"):
    dtype, down = {"e4m3": (ml_dtypes.float8_e4m3fn, 7), "e5m2": (ml_dtypes.float8_e5m2, 14)}[fmt]
    v = np.moveaxis(np.asarray(x, np.float32).astype(ml_dtypes.bfloat16).astype(np.float64), axis, -1)
    blocks = v.reshape(v.shape[:-1] + (-1, 32))
    amax = np.abs(blocks).max(-1, keepdims=True)
    byte = np.maximum(np.where(amax > 0, np.frexp(amax)[1] - 1 + 127, 0) - down, 1)
    scale = np.exp2(byte - 127.0)
    codes = (blocks / scale).astype(np.float32).astype(dtype).astype(np.float64)
    return np.moveaxis((codes * scale).reshape(v.shape), -1, axis)


WIDE = False


def mx_kscale(k):
    if not WIDE:
        return np.ones(k)
    levels = np.array([10, -10, 5, -5, 0])
    if k % 512:
        return np.exp2(np.random.permutation(np.resize(levels, k // 32))).repeat(32)
    a = np.empty((k // 512, 16))
    for p in range(k // 512):
        a[p, :8] = np.random.permutation(np.resize(levels, 8))
        for g in range(8):
            far = levels[np.abs(levels - a[p, g]) >= 10]
            a[p, g + 8] = far[np.random.randint(len(far))]
    return np.exp2(a.ravel()).repeat(32)


def f64(x):
    return np.asarray(x).astype(np.float64)


def striped(idx):
    return np.tile(idx.reshape(-1, 16).T, (8, 1)).astype(np.uint16)


def unstriped(offs):
    return offs[:16].T.reshape(-1).astype(np.int64)


def pack_weight(w):
    k, n = w.shape
    w = f64(np.asarray(w, np.float32).astype(ml_dtypes.bfloat16)).reshape(k // 32, 32, n)
    amax = np.abs(w).max(1)
    byte = np.clip(np.where(amax > 0, np.frexp(amax)[1] - 1 + 127 - 7, 1), 1, 254)
    scaled = (w * np.exp2(127.0 - byte)[:, None, :]).reshape(k, n).astype(np.float32)
    words = np.ascontiguousarray(scaled.reshape(k // 512, 128, 4, n).transpose(0, 1, 3, 2)).astype(ml_dtypes.float8_e4m3fn).view(np.uint8)
    return words, np.ascontiguousarray(byte.astype(np.uint8).reshape(k // 512, 16, n))


def unpack_weight(words, scales):
    g, p, n, _ = words.shape
    vals = np.ascontiguousarray(words).view(ml_dtypes.float8_e4m3fn).astype(np.float64) * np.repeat(np.exp2(scales.astype(np.float64) - 127.0), 8, axis=1)[..., None]
    return vals.transpose(0, 1, 3, 2).reshape(g * 512, n)


K, T, S, D, N, H, V, U = 512, 2048, 1024, 4, 128, 512, 256, 512


def setup_inputs():
    n = np.random.standard_normal
    s = mx_kscale(K)[:, None]
    u = mx_kscale(H)
    packed_xT = pack_weight(n((K, T)) * s)
    return {
        "x_words": packed_xT[0],
        "x_scales": packed_xT[1],
        "w1": (n((K, H)) / np.sqrt(K) / s).astype(np.float32),
        "tau": (np.random.uniform(0.5, 1.0, (H, S))).astype(np.float32),
        "df0": (np.random.uniform(0.6, 1.0, (H, S))).astype(np.float32),
        "strk": (np.random.uniform(0.1, 0.5, (H, U))).astype(np.float32),
        "unit": (np.random.uniform(0.6, 1.4, (H, 1)) * u[:, None]).astype(np.float32),
        "w2": (n((H, N)) / np.sqrt(H) / u[:, None]).astype(np.float32),
        "offs": striped(np.random.permutation(T)[:S]),
        "opt": striped(np.random.permutation(np.concatenate([np.arange(V), np.random.randint(0, V, U - V)]))),
    }


def reference(x_words, x_scales, w1, tau, df0, strk, unit, w2, offs, opt):
    xq = unpack_weight(x_words, x_scales)[:, unstriped(offs)]
    fw = mxq(f64(w1), 0, "e4m3").T @ xq
    fwd = 0.3 * (np.log(np.exp(fw) + 1.0))
    grow = fwd * f64(tau) + 1.0
    df = f64(df0) / grow
    ann = df.reshape(len(df), -1, D).sum(axis=2)
    ao = ann[:, unstriped(opt)]
    leg = df * fwd
    flt = leg.reshape(len(leg), -1, D).sum(axis=2)
    swp = flt / ann
    so = swp[:, unstriped(opt)]
    mny = 4.0 * (so - f64(strk))
    sp2 = np.log(np.exp(mny) + 1.0)
    hid = f64(unit) * (ao * sp2)
    return mxq(f64(w2), 0, "e4m3").T @ mxq(hid, 0, "e4m3")

@@ -1,0 +1,235 @@
+from contextlib import ExitStack
+
+import concourse.mybir as mybir
+
+F32 = mybir.dt.float32
+BF16 = mybir.dt.bfloat16
+I32 = mybir.dt.int32
+U32 = mybir.dt.uint32
+U16 = mybir.dt.uint16
+U8 = mybir.dt.uint8
+FP8X4 = mybir.dt.float8_e4m3fn_x4
+ALU = mybir.AluOpType
+ACT = mybir.ActivationFunctionType
+
+P = 128
+PACK = 4
+T, S, H, V, U, N = 2048, 1024, 512, 256, 512, 128
+BANK = 512
+HALVES = S // BANK
+WINDOW = 528
+CHUNK = 128
+SCALAR_GATHERS = 2
+TINY = 2.0 ** -60
+
+FLOPS = 2 * 512 * 512 * 1024 + 2 * 512 * 128 * 512
+
+
+def tile_picked_yswapa_val_p_kernel(
+    tc, x_words, x_scales, w1, tau, df0, strk, unit, w2, offs, opt, out
+):
+    nc = tc.nc
+    with ExitStack() as ctx:
+        keep = ctx.enter_context(tc.tile_pool(name="keep", bufs=1))
+        psum = ctx.enter_context(tc.psum_pool(name="psum", bufs=8))
+
+        def sb(name, shape, dtype, reuse=None):
+            return keep.tile(shape, dtype, name=name, tag=reuse or name, align_bytes=64)
+
+        offs_sb = keep.tile([P, S // 16], U16, name="offs_sb")
+        opt_sb = keep.tile([P, U // 16], U16, name="opt_sb")
+        node_words = sb("node_words", [P, T], I32)
+        node_scales = sb("node_scales", [P, T], U8)
+        w1_raw = sb("w1_raw", [P, PACK, H], F32)
+        consts = sb("consts", [P, 2], F32)
+
+        nc.vector.memset(node_scales[:].bitcast(I32), 0)
+        nc.sync.dma_start(offs_sb[:], offs)
+        for q in range(4):
+            nc.scalar.dma_start(
+                node_scales[32 * q : 32 * q + 4, :].bitcast(I32),
+                x_scales[0, 4 * q : 4 * q + 4, :].bitcast(I32),
+            )
+        nc.sync.dma_start(w1_raw[:], w1.rearrange("(p j) c -> p j c", j=PACK))
+        nc.sync.dma_start(node_words[:], x_words[0].rearrange("p n j -> p (n j)").bitcast(I32))
+        nc.sync.dma_start(opt_sb[:], opt)
+
+        nc.vector.memset(consts[:, 0:1], TINY)
+        nc.vector.memset(consts[:, 1:2], 1.0)
+        tiny, one = consts[:, 0:1], consts[:, 1:2]
+        ann_win = [sb(f"ann_win{t}", [P, WINDOW], F32) for t in range(PACK)]
+        swp_win = [sb(f"swp_win{t}", [P, WINDOW], F32) for t in range(PACK)]
+        for win in ann_win + swp_win:
+            nc.vector.memset(win[:, V:], 0.0)
+
+        cols = BANK // 16
+        picked_scales = [sb(f"picked_scales{h}", [P, BANK], U8) for h in range(HALVES)]
+        picked_words = [sb(f"picked_words{h}", [P, BANK], U32) for h in range(HALVES)]
+        for h in range(HALVES):
+            nc.vector.tensor_copy(
+                picked_scales[h][:], node_scales[:].indirect(offs_sb[:, h * cols : (h + 1) * cols])
+            )
+        tau_sb = sb("tau_sb", [P, PACK, S], F32, reuse="node_scales")
+        nc.sync.dma_start(tau_sb[:], tau.rearrange("(p t) j -> p t j", t=PACK))
+        w1_bf = sb("w1_bf", [P, PACK * H], BF16)
+        w1_codes = sb("w1_codes", [P, H], U32)
+        w1_scales = sb("w1_scales", [P, H], U8)
+        nc.vector.tensor_copy(
+            w1_bf[:].rearrange("p (t m j) -> p m t j", t=PACK, j=PACK),
+            w1_raw[:].rearrange("p j (m t) -> p m t j", t=PACK),
+        )
+        nc.vector.quantize_mx(out=w1_codes[:].bitcast(FP8X4), scales=w1_scales[:], in_=w1_bf[:])
+        df0_sb = sb("df0_sb", [P, PACK, S], F32, reuse="w1_raw")
+        nc.sync.dma_start(df0_sb[:], df0.rearrange("(p t) j -> p t j", t=PACK))
+        w2_raw = sb("w2_raw", [P, PACK, N], F32, reuse="w1_bf")
+        nc.sync.dma_start(w2_raw[:], w2.rearrange("(p j) m -> p j m", j=PACK))
+        for h in range(HALVES):
+            nc.vector.tensor_copy(
+                picked_words[h][:],
+                node_words[:].bitcast(U32).indirect(offs_sb[:, h * cols : (h + 1) * cols]),
+            )
+
+        strk_sb = sb("strk_sb", [P, PACK, U], F32, reuse="node_words")
+        nc.sync.dma_start(strk_sb[:], strk.rearrange("(p t) r -> p t r", t=PACK))
+
+        fw = {}
+        logsig = [sb(f"logsig{t}", [P, S], F32) for t in range(PACK)]
+        sig = [sb(f"sig{t}", [P, S], F32) for t in range(PACK)]
+        for h in range(HALVES):
+            for t in range(PACK):
+                fw[t, h] = psum.tile([P, BANK], F32, name="bank")
+                nc.tensor.matmul_mx(
+                    out=fw[t, h][:],
+                    lhsT=w1_codes[:, t * P : (t + 1) * P].bitcast(FP8X4),
+                    lhsT_scale=w1_scales[:, t * P : (t + 1) * P],
+                    rhs=picked_words[h][:].bitcast(FP8X4),
+                    rhs_scale=picked_scales[h][:],
+                    start=True,
+                    stop=True,
+                )
+                nc.scalar.activation(
+                    sig[t][:, h * BANK : (h + 1) * BANK], fw[t, h][:], ACT.Sigmoid, scale=-1.0
+                )
+
+        unit_sb = sb("unit_sb", [P, PACK], F32, reuse="picked_scales0")
+        nc.sync.dma_start(unit_sb[:], unit.rearrange("(p t) o -> p (t o)", t=PACK))
+        w2_bf = sb("w2_bf", [P, N, PACK], BF16)
+        w2_codes = sb("w2_codes", [P, N], U32)
+        w2_scales = sb("w2_scales", [P, N], U8)
+        nc.vector.tensor_copy(w2_bf[:], w2_raw[:].rearrange("p j m -> p m j"))
+        nc.vector.quantize_mx(
+            out=w2_codes[:].bitcast(FP8X4),
+            scales=w2_scales[:],
+            in_=w2_bf[:].rearrange("p m j -> p (m j)"),
+        )
+
+        soft = [sb(f"soft{t}", [P, S], F32) for t in range(PACK)]
+        accr = [sb(f"accr{t}", [P, S], F32) for t in range(PACK)]
+        for t in range(PACK):
+            nc.scalar.activation(logsig[t][:], sig[t][:], ACT.Ln, bias=tiny)
+            for h in range(HALVES):
+                hs = slice(h * BANK, (h + 1) * BANK)
+                nc.vector.scalar_tensor_tensor(
+                    soft[t][:, hs], logsig[t][:, hs], -1.0, fw[t, h][:], ALU.mult, ALU.max
+                )
+            nc.vector.tensor_tensor(accr[t][:], soft[t][:], tau_sb[:, t, :], ALU.mult)
+
+        df = sig
+        ann = sb("ann", [P, PACK, V], F32)
+        ann_root = sb("ann_root", [P, PACK, V], F32)
+        ann_inv = sb("ann_inv", [P, PACK, V], F32)
+        pairs = [sb(f"pairs{t}", [P, S // 2], F32) for t in range(PACK)]
+        for t in range(PACK):
+            root, inv = sig[t], logsig[t]
+            nc.scalar.activation(root[:], accr[t][:], ACT.Abs_reciprocal_sqrt, bias=one, scale=0.3)
+            nc.scalar.activation(inv[:], root[:], ACT.Square)
+            nc.vector.tensor_tensor(df[t][:], inv[:], df0_sb[:, t, :], ALU.mult)
+            nc.vector.tensor_tensor(pairs[t][:], df[t][:, 0::2], df[t][:, 1::2], ALU.add)
+            nc.vector.tensor_tensor(ann[:, t, :], pairs[t][:, 0::2], pairs[t][:, 1::2], ALU.add)
+        for t in range(PACK):
+            nc.scalar.activation(ann_root[:, t, :], ann[:, t, :], ACT.Abs_reciprocal_sqrt)
+        nc.scalar.activation(ann_inv[:], ann_root[:], ACT.Square)
+
+        flt = sb("flt", [P, PACK, V], F32)
+        weight = sb("weight", [P, PACK, U], F32)
+        gap = sb("gap", [P, PACK, U], F32)
+        sig2 = sb("sig2", [P, PACK, U], F32)
+        swp_picked = [sb(f"swp_picked{t}", [P, U], F32) for t in range(SCALAR_GATHERS)]
+        for t in range(PACK):
+            nc.vector.tensor_scalar(
+                ann_win[t][:, :V], ann[:, t, :], unit_sb[:, t : t + 1], -4.0, ALU.mult, ALU.mult
+            )
+            nc.scalar.activation(weight[:, t, :], ann_win[t][:].indirect(opt_sb[:]), ACT.Copy)
+        for t in range(PACK):
+            leg = accr[t]
+            nc.vector.tensor_tensor(leg[:], df[t][:], soft[t][:], ALU.mult)
+            nc.vector.tensor_tensor(pairs[t][:], leg[:, 0::2], leg[:, 1::2], ALU.add)
+            nc.vector.tensor_tensor(flt[:, t, :], pairs[t][:, 0::2], pairs[t][:, 1::2], ALU.add)
+            nc.vector.scalar_tensor_tensor(
+                swp_win[t][:, :V], flt[:, t, :], -0.3, ann_inv[:, t, :], ALU.mult, ALU.mult
+            )
+            if t < SCALAR_GATHERS:
+                nc.scalar.activation(swp_picked[t][:], swp_win[t][:].indirect(opt_sb[:]), ACT.Copy)
+                nc.vector.tensor_tensor(gap[:, t, :], swp_picked[t][:], strk_sb[:, t, :], ALU.add)
+            else:
+                nc.vector.tensor_tensor(
+                    gap[:, t, :], swp_win[t][:].indirect(opt_sb[:]), strk_sb[:, t, :], ALU.add
+                )
+            nc.scalar.activation(sig2[:, t, :], gap[:, t, :], ACT.Sigmoid, scale=4.0)
+
+        weight_il = sb("weight_il", [P, U, PACK], F32)
+        gap_il = sb("gap_il", [P, U, PACK], F32)
+        nc.vector.tensor_copy(gap_il[:], gap[:].rearrange("p t r -> p r t"))
+        nc.vector.tensor_copy(weight_il[:], weight[:].rearrange("p t r -> p r t"))
+        chunks = U // CHUNK
+        logsig2 = [sb(f"logsig2_{c}", [P, CHUNK, PACK], F32) for c in range(chunks)]
+        payoff = [sb(f"payoff{c}", [P, CHUNK * PACK], F32) for c in range(chunks)]
+        hid = [sb(f"hid{c}", [P, CHUNK * PACK], BF16) for c in range(chunks)]
+        hid_codes = [sb(f"hid_codes{c}", [P, CHUNK], U32) for c in range(chunks)]
+        hid_scales = [sb(f"hid_scales{c}", [P, CHUNK], U8) for c in range(chunks)]
+        result = [sb(f"result{c}", [P, CHUNK], F32) for c in range(chunks)]
+
+        def rows(tile, c):
+            return tile[:, c * CHUNK : (c + 1) * CHUNK, :].rearrange("p r t -> p (r t)")
+
+        def take_payoff(c):
+            nc.scalar.activation(
+                logsig2[c][:],
+                sig2[:, :, c * CHUNK : (c + 1) * CHUNK].rearrange("p t r -> p r t"),
+                ACT.Ln,
+                bias=tiny,
+            )
+            nc.vector.scalar_tensor_tensor(
+                payoff[c][:],
+                logsig2[c][:].rearrange("p r t -> p (r t)"),
+                0.25,
+                rows(gap_il, c),
+                ALU.mult,
+                ALU.min,
+            )
+
+        def weigh(c):
+            nc.vector.tensor_tensor(hid[c][:], payoff[c][:], rows(weight_il, c), ALU.mult)
+
+        def book(c):
+            nc.vector.quantize_mx(out=hid_codes[c][:].bitcast(FP8X4), scales=hid_scales[c][:], in_=hid[c][:])
+            acc = psum.tile([P, BANK], F32, name="bank")
+            nc.tensor.matmul_mx(
+                out=acc[:, :CHUNK],
+                lhsT=w2_codes[:].bitcast(FP8X4),
+                lhsT_scale=w2_scales[:],
+                rhs=hid_codes[c][:].bitcast(FP8X4),
+                rhs_scale=hid_scales[c][:],
+                start=True,
+                stop=True,
+            )
+            nc.scalar.copy(result[c][:], acc[:, :CHUNK])
+            nc.sync.dma_start(out[:, c * CHUNK : (c + 1) * CHUNK], result[c][:])
+
+        for step in range(chunks + 2):
+            if step < chunks:
+                take_payoff(step)
+            if 1 <= step <= chunks:
+                weigh(step - 1)
+            if step >= 2:
+                book(step - 2)

@@ -1,6 +1,7 @@
 from contextlib import ExitStack
 
 import concourse.mybir as mybir
+from concourse.masks import make_identity
 
 F32 = mybir.dt.float32
 BF16 = mybir.dt.bfloat16
@@ -19,7 +20,9 @@ BANK = 512
 HALVES = S // BANK
 WINDOW = 528
 CHUNK = 128
+WIDE_WINDOW = 1024
 SCALAR_GATHERS = 2
+D = 4
 TINY = 2.0 ** -60
 
 FLOPS = 2 * 512 * 512 * 1024 + 2 * 512 * 128 * 512
@@ -40,37 +43,63 @@ def tile_picked_yswapa_val_p_kernel(
         opt_sb = keep.tile([P, U // 16], U16, name="opt_sb")
         node_words = sb("node_words", [P, T], I32)
         node_scales = sb("node_scales", [P, T], U8)
+        scale_rows = sb("scale_rows", [P, T], U8)
+        ident = sb("ident", [P, P], F32)
         w1_raw = sb("w1_raw", [P, PACK, H], F32)
         consts = sb("consts", [P, 2], F32)
 
         nc.vector.memset(node_scales[:].bitcast(I32), 0)
         nc.sync.dma_start(offs_sb[:], offs)
         for q in range(4):
-            nc.scalar.dma_start(
-                node_scales[32 * q : 32 * q + 4, :].bitcast(I32),
+            nc.sync.dma_start(
+                scale_rows[32 * q : 32 * q + 4, :].bitcast(I32),
                 x_scales[0, 4 * q : 4 * q + 4, :].bitcast(I32),
             )
         nc.sync.dma_start(w1_raw[:], w1.rearrange("(p j) c -> p j c", j=PACK))
         nc.sync.dma_start(node_words[:], x_words[0].rearrange("p n j -> p (n j)").bitcast(I32))
         nc.sync.dma_start(opt_sb[:], opt)
+        w2_raw = sb("w2_raw", [P, PACK, N], F32)
+        nc.sync.dma_start(w2_raw[:], w2.rearrange("(p j) m -> p j m", j=PACK))
+        unit_sb = sb("unit_sb", [P, PACK], F32)
+        nc.sync.dma_start(unit_sb[:], unit.rearrange("(p t) o -> p (t o)", t=PACK))
 
         nc.vector.memset(consts[:, 0:1], TINY)
         nc.vector.memset(consts[:, 1:2], 1.0)
         tiny, one = consts[:, 0:1], consts[:, 1:2]
-        ann_win = [sb(f"ann_win{t}", [P, WINDOW], F32) for t in range(PACK)]
+        ann_win = [
+            sb(f"ann_win{t}", [P, WINDOW if t < SCALAR_GATHERS else WIDE_WINDOW], F32)
+            for t in range(PACK)
+        ]
         swp_win = [sb(f"swp_win{t}", [P, WINDOW], F32) for t in range(PACK)]
         for win in ann_win + swp_win:
             nc.vector.memset(win[:, V:], 0.0)
 
+        make_identity(nc, ident[:])
+        for q in range(4):
+            nc.vector.tensor_copy(
+                node_scales[32 * q : 32 * q + 4, :].bitcast(I32),
+                scale_rows[32 * q : 32 * q + 4, :].bitcast(I32),
+            )
+        tau_raw = sb("tau_raw", [P, PACK, S], F32, reuse="scale_rows")
+        nc.sync.dma_start(tau_raw[:], tau.rearrange("(p t) j -> p t j", t=PACK))
+
         cols = BANK // 16
-        picked_scales = [sb(f"picked_scales{h}", [P, BANK], U8) for h in range(HALVES)]
-        picked_words = [sb(f"picked_words{h}", [P, BANK], U32) for h in range(HALVES)]
-        for h in range(HALVES):
+        picked_scales, picked_words = [], []
+
+        def pick_scales(h, reuse=None):
+            picked_scales.append(sb(f"picked_scales{h}", [P, BANK], U8, reuse=reuse))
             nc.vector.tensor_copy(
                 picked_scales[h][:], node_scales[:].indirect(offs_sb[:, h * cols : (h + 1) * cols])
             )
-        tau_sb = sb("tau_sb", [P, PACK, S], F32, reuse="node_scales")
-        nc.sync.dma_start(tau_sb[:], tau.rearrange("(p t) j -> p t j", t=PACK))
+
+        def pick_words(h):
+            picked_words.append(sb(f"picked_words{h}", [P, BANK], U32))
+            nc.vector.tensor_copy(
+                picked_words[h][:],
+                node_words[:].bitcast(U32).indirect(offs_sb[:, h * cols : (h + 1) * cols]),
+            )
+
+        pick_scales(0)
         w1_bf = sb("w1_bf", [P, PACK * H], BF16)
         w1_codes = sb("w1_codes", [P, H], U32)
         w1_scales = sb("w1_scales", [P, H], U8)
@@ -79,18 +108,29 @@ def tile_picked_yswapa_val_p_kernel(
             w1_raw[:].rearrange("p j (m t) -> p m t j", t=PACK),
         )
         nc.vector.quantize_mx(out=w1_codes[:].bitcast(FP8X4), scales=w1_scales[:], in_=w1_bf[:])
-        df0_sb = sb("df0_sb", [P, PACK, S], F32, reuse="w1_raw")
-        nc.sync.dma_start(df0_sb[:], df0.rearrange("(p t) j -> p t j", t=PACK))
-        w2_raw = sb("w2_raw", [P, PACK, N], F32, reuse="w1_bf")
-        nc.sync.dma_start(w2_raw[:], w2.rearrange("(p j) m -> p j m", j=PACK))
-        for h in range(HALVES):
-            nc.vector.tensor_copy(
-                picked_words[h][:],
-                node_words[:].bitcast(U32).indirect(offs_sb[:, h * cols : (h + 1) * cols]),
-            )
+        pick_words(0)
+        pick_scales(1, reuse="w1_bf")
+        pick_words(1)
+        df0_rows = df0.rearrange("(p t) j -> p t j", t=PACK)
+        df0_raw = []
+        for u, spent in enumerate(("w1_raw", "node_scales")):
+            df0_raw.append(sb(f"df0_raw{u}", [P, 2, S], F32, reuse=spent))
+            nc.sync.dma_start(df0_raw[u][:], df0_rows[:, 2 * u : 2 * u + 2, :])
 
         strk_sb = sb("strk_sb", [P, PACK, U], F32, reuse="node_words")
         nc.sync.dma_start(strk_sb[:], strk.rearrange("(p t) r -> p t r", t=PACK))
+
+        def planes(tile, h):
+            return tile[:, h * BANK : (h + 1) * BANK].rearrange("p (d v) -> p d v", d=D)
+
+        def by_period(bank):
+            return bank[:].rearrange("p (v d) -> p d v", d=D)
+
+        def split_periods(dst, src):
+            nc.vector.tensor_copy(
+                dst.rearrange("p (h d v) -> p h v d", h=HALVES, d=D),
+                src.rearrange("p (h v d) -> p h v d", h=HALVES, d=D),
+            )
 
         fw = {}
         logsig = [sb(f"logsig{t}", [P, S], F32) for t in range(PACK)]
@@ -108,11 +148,9 @@ def tile_picked_yswapa_val_p_kernel(
                     stop=True,
                 )
                 nc.scalar.activation(
-                    sig[t][:, h * BANK : (h + 1) * BANK], fw[t, h][:], ACT.Sigmoid, scale=-1.0
+                    planes(sig[t], h), by_period(fw[t, h]), ACT.Sigmoid, scale=-1.0
                 )
 
-        unit_sb = sb("unit_sb", [P, PACK], F32, reuse="picked_scales0")
-        nc.sync.dma_start(unit_sb[:], unit.rearrange("(p t) o -> p (t o)", t=PACK))
         w2_bf = sb("w2_bf", [P, N, PACK], BF16)
         w2_codes = sb("w2_codes", [P, N], U32)
         w2_scales = sb("w2_scales", [P, N], U8)
@@ -123,67 +161,139 @@ def tile_picked_yswapa_val_p_kernel(
             in_=w2_bf[:].rearrange("p m j -> p (m j)"),
         )
 
+        unit4 = sb("unit4", [P, PACK], F32)
+        nc.vector.tensor_scalar(unit4[:], unit_sb[:], -4.0, None, ALU.mult)
+
         soft = [sb(f"soft{t}", [P, S], F32) for t in range(PACK)]
         accr = [sb(f"accr{t}", [P, S], F32) for t in range(PACK)]
+        tau_sb = [sb(f"tau{t}", [P, S], F32) for t in range(PACK)]
+        for t in range(PACK):
+            split_periods(tau_sb[t][:], tau_raw[:, t, :])
         for t in range(PACK):
             nc.scalar.activation(logsig[t][:], sig[t][:], ACT.Ln, bias=tiny)
             for h in range(HALVES):
-                hs = slice(h * BANK, (h + 1) * BANK)
                 nc.vector.scalar_tensor_tensor(
-                    soft[t][:, hs], logsig[t][:, hs], -1.0, fw[t, h][:], ALU.mult, ALU.max
+                    planes(soft[t], h),
+                    planes(logsig[t], h),
+                    -1.0,
+                    by_period(fw[t, h]),
+                    ALU.mult,
+                    ALU.max,
                 )
-            nc.vector.tensor_tensor(accr[t][:], soft[t][:], tau_sb[:, t, :], ALU.mult)
+            nc.vector.tensor_tensor(accr[t][:], soft[t][:], tau_sb[t][:], ALU.mult)
 
-        df = sig
-        ann = sb("ann", [P, PACK, V], F32)
-        ann_root = sb("ann_root", [P, PACK, V], F32)
-        ann_inv = sb("ann_inv", [P, PACK, V], F32)
-        pairs = [sb(f"pairs{t}", [P, S // 2], F32) for t in range(PACK)]
-        for t in range(PACK):
-            root, inv = sig[t], logsig[t]
+        def sum_periods(bank, slot, tile):
+            for h in range(HALVES):
+                block = slot * HALVES + h
+                for d in range(D):
+                    nc.tensor.matmul(
+                        bank[:, block * P : (block + 1) * P],
+                        planes(tile, h)[:, d, :],
+                        ident[:],
+                        start=(d == 0),
+                        stop=(d == D - 1),
+                        is_transpose=True,
+                    )
+
+        def turn_back(name, bank):
+            turned = sb(name, [P, BANK], F32)
+            nc.scalar.copy(turned[:], bank[:])
+            back = psum.tile([P, BANK], F32, name="bank")
+            for block in range(BANK // P):
+                cs = slice(block * P, (block + 1) * P)
+                nc.tensor.transpose(back[:, cs], turned[:, cs], ident[:])
+            return back
+
+        df0_sb = [sb(f"df0_{t}", [P, S], F32) for t in range(PACK)]
+        ann_root = sb("ann_root", [P, PACK * V], F32)
+        ann_inv = sb("ann_inv", [P, PACK * V], F32)
+        gap = sb("gap", [P, PACK, U], F32)
+        sums = {}
+
+        def discount(t):
+            u, slot = divmod(t, 2)
+            if slot == 0:
+                sums["ann", u] = psum.tile([P, BANK], F32, name="bank")
+                sums["flt", u] = psum.tile([P, BANK], F32, name="bank")
+            root, inv, df = sig[t], logsig[t], sig[t]
+            split_periods(df0_sb[t][:], df0_raw[u][:, slot, :])
             nc.scalar.activation(root[:], accr[t][:], ACT.Abs_reciprocal_sqrt, bias=one, scale=0.3)
             nc.scalar.activation(inv[:], root[:], ACT.Square)
-            nc.vector.tensor_tensor(df[t][:], inv[:], df0_sb[:, t, :], ALU.mult)
-            nc.vector.tensor_tensor(pairs[t][:], df[t][:, 0::2], df[t][:, 1::2], ALU.add)
-            nc.vector.tensor_tensor(ann[:, t, :], pairs[t][:, 0::2], pairs[t][:, 1::2], ALU.add)
-        for t in range(PACK):
-            nc.scalar.activation(ann_root[:, t, :], ann[:, t, :], ACT.Abs_reciprocal_sqrt)
-        nc.scalar.activation(ann_inv[:], ann_root[:], ACT.Square)
+            nc.vector.tensor_tensor(df[:], inv[:], df0_sb[t][:], ALU.mult)
+            sum_periods(sums["ann", u], slot, df)
 
-        flt = sb("flt", [P, PACK, V], F32)
-        weight = sb("weight", [P, PACK, U], F32)
-        gap = sb("gap", [P, PACK, U], F32)
-        sig2 = sb("sig2", [P, PACK, U], F32)
-        swp_picked = [sb(f"swp_picked{t}", [P, U], F32) for t in range(SCALAR_GATHERS)]
-        for t in range(PACK):
-            nc.vector.tensor_scalar(
-                ann_win[t][:, :V], ann[:, t, :], unit_sb[:, t : t + 1], -4.0, ALU.mult, ALU.mult
-            )
-            nc.scalar.activation(weight[:, t, :], ann_win[t][:].indirect(opt_sb[:]), ACT.Copy)
-        for t in range(PACK):
-            leg = accr[t]
-            nc.vector.tensor_tensor(leg[:], df[t][:], soft[t][:], ALU.mult)
-            nc.vector.tensor_tensor(pairs[t][:], leg[:, 0::2], leg[:, 1::2], ALU.add)
-            nc.vector.tensor_tensor(flt[:, t, :], pairs[t][:, 0::2], pairs[t][:, 1::2], ALU.add)
-            nc.vector.scalar_tensor_tensor(
-                swp_win[t][:, :V], flt[:, t, :], -0.3, ann_inv[:, t, :], ALU.mult, ALU.mult
-            )
-            if t < SCALAR_GATHERS:
-                nc.scalar.activation(swp_picked[t][:], swp_win[t][:].indirect(opt_sb[:]), ACT.Copy)
-                nc.vector.tensor_tensor(gap[:, t, :], swp_picked[t][:], strk_sb[:, t, :], ALU.add)
-            else:
+        def float_leg(t):
+            u, slot = divmod(t, 2)
+            df, leg = sig[t], accr[t]
+            nc.vector.tensor_tensor(leg[:], df[:], soft[t][:], ALU.mult)
+            sum_periods(sums["flt", u], slot, leg)
+
+        def invert_annuity(u, ann):
+            us = slice(u * BANK, (u + 1) * BANK)
+            nc.scalar.activation(ann_root[:, us], ann[:], ACT.Abs_reciprocal_sqrt)
+            nc.scalar.activation(ann_inv[:, us], ann_root[:, us], ACT.Square)
+
+        def scale_annuity(u, ann):
+            for slot in range(2):
+                t = 2 * u + slot
+                nc.scalar.activation(
+                    ann_win[t][:, :V],
+                    ann[:, slot * V : (slot + 1) * V],
+                    ACT.Copy,
+                    scale=unit4[:, t : t + 1],
+                )
+
+        def moneyness(u, flt):
+            for slot in range(2):
+                t = 2 * u + slot
+                nc.vector.scalar_tensor_tensor(
+                    swp_win[t][:, :V],
+                    flt[:, slot * V : (slot + 1) * V],
+                    -0.3,
+                    ann_inv[:, t * V : (t + 1) * V],
+                    ALU.mult,
+                    ALU.mult,
+                )
+            for slot in range(2):
+                t = 2 * u + slot
                 nc.vector.tensor_tensor(
                     gap[:, t, :], swp_win[t][:].indirect(opt_sb[:]), strk_sb[:, t, :], ALU.add
                 )
-            nc.scalar.activation(sig2[:, t, :], gap[:, t, :], ACT.Sigmoid, scale=4.0)
 
-        weight_il = sb("weight_il", [P, U, PACK], F32)
-        gap_il = sb("gap_il", [P, U, PACK], F32)
+        for t in range(2):
+            discount(t)
+            float_leg(t)
+        discount(2)
+        discount(3)
+        ann0 = turn_back("ann_turned0", sums["ann", 0])
+        flt0 = turn_back("flt_turned0", sums["flt", 0])
+        invert_annuity(0, ann0)
+        float_leg(2)
+        ann1 = turn_back("ann_turned1", sums["ann", 1])
+        float_leg(3)
+        flt1 = turn_back("flt_turned1", sums["flt", 1])
+        invert_annuity(1, ann1)
+        moneyness(0, flt0)
+        moneyness(1, flt1)
+        scale_annuity(0, ann0)
+        scale_annuity(1, ann1)
+
+        sig2 = sb("sig2", [P, PACK, U], F32, reuse="ann_root")
+        for t in range(PACK):
+            nc.scalar.activation(sig2[:, t, :], gap[:, t, :], ACT.Sigmoid, scale=4.0)
+        weight = sb("weight", [P, PACK, U], F32, reuse="node_words")
+        for t in range(SCALAR_GATHERS):
+            nc.scalar.activation(weight[:, t, :], ann_win[t][:].indirect(opt_sb[:]), ACT.Copy)
+
+        weight_il = sb("weight_il", [P, U, PACK], F32, reuse="w1_raw")
+        gap_il = sb("gap_il", [P, U, PACK], F32, reuse="scale_rows")
         nc.vector.tensor_copy(gap_il[:], gap[:].rearrange("p t r -> p r t"))
+        for t in range(SCALAR_GATHERS, PACK):
+            nc.vector.tensor_copy(weight[:, t, :], ann_win[t][:].indirect(opt_sb[:]))
         nc.vector.tensor_copy(weight_il[:], weight[:].rearrange("p t r -> p r t"))
         chunks = U // CHUNK
-        logsig2 = [sb(f"logsig2_{c}", [P, CHUNK, PACK], F32) for c in range(chunks)]
-        payoff = [sb(f"payoff{c}", [P, CHUNK * PACK], F32) for c in range(chunks)]
+        logsig2 = [sb(f"logsig2_{c}", [P, CHUNK, PACK], F32, reuse=f"tau{c}") for c in range(chunks)]
+        payoff = [sb(f"payoff{c}", [P, CHUNK * PACK], F32, reuse=f"df0_{c}") for c in range(chunks)]
         hid = [sb(f"hid{c}", [P, CHUNK * PACK], BF16) for c in range(chunks)]
         hid_codes = [sb(f"hid_codes{c}", [P, CHUNK], U32) for c in range(chunks)]
         hid_scales = [sb(f"hid_scales{c}", [P, CHUNK], U8) for c in range(chunks)]

@@ -18,9 +18,9 @@ PACK = 4
 T, S, H, V, U, N = 2048, 1024, 512, 256, 512, 128
 BANK = 512
 HALVES = S // BANK
-WINDOW = 528
+WINDOW = 272
 CHUNK = 128
-WIDE_WINDOW = 1024
+PIECE = 256
 SCALAR_GATHERS = 2
 D = 4
 TINY = 2.0 ** -60
@@ -66,10 +66,7 @@ def tile_picked_yswapa_val_p_kernel(
         nc.vector.memset(consts[:, 0:1], TINY)
         nc.vector.memset(consts[:, 1:2], 1.0)
         tiny, one = consts[:, 0:1], consts[:, 1:2]
-        ann_win = [
-            sb(f"ann_win{t}", [P, WINDOW if t < SCALAR_GATHERS else WIDE_WINDOW], F32)
-            for t in range(PACK)
-        ]
+        ann_win = [sb(f"ann_win{t}", [P, WINDOW], F32) for t in range(PACK)]
         swp_win = [sb(f"swp_win{t}", [P, WINDOW], F32) for t in range(PACK)]
         for win in ann_win + swp_win:
             nc.vector.memset(win[:, V:], 0.0)
@@ -81,7 +78,9 @@ def tile_picked_yswapa_val_p_kernel(
                 scale_rows[32 * q : 32 * q + 4, :].bitcast(I32),
             )
         tau_raw = sb("tau_raw", [P, PACK, S], F32, reuse="scale_rows")
-        nc.sync.dma_start(tau_raw[:], tau.rearrange("(p t) j -> p t j", t=PACK))
+        tau_rows = tau.rearrange("(p t) j -> p t j", t=PACK)
+        for u in range(2):
+            nc.sync.dma_start(tau_raw[:, 2 * u : 2 * u + 2, :], tau_rows[:, 2 * u : 2 * u + 2, :])
 
         cols = BANK // 16
         picked_scales, picked_words = [], []
@@ -104,8 +103,8 @@ def tile_picked_yswapa_val_p_kernel(
         w1_codes = sb("w1_codes", [P, H], U32)
         w1_scales = sb("w1_scales", [P, H], U8)
         nc.vector.tensor_copy(
-            w1_bf[:].rearrange("p (t m j) -> p m t j", t=PACK, j=PACK),
-            w1_raw[:].rearrange("p j (m t) -> p m t j", t=PACK),
+            w1_bf[:].rearrange("p (t m j) -> p m j t", t=PACK, j=PACK),
+            w1_raw[:].rearrange("p j (m t) -> p m j t", t=PACK),
         )
         nc.vector.quantize_mx(out=w1_codes[:].bitcast(FP8X4), scales=w1_scales[:], in_=w1_bf[:])
         pick_words(0)
@@ -115,7 +114,8 @@ def tile_picked_yswapa_val_p_kernel(
         df0_raw = []
         for u, spent in enumerate(("w1_raw", "node_scales")):
             df0_raw.append(sb(f"df0_raw{u}", [P, 2, S], F32, reuse=spent))
-            nc.sync.dma_start(df0_raw[u][:], df0_rows[:, 2 * u : 2 * u + 2, :])
+            for slot in range(2):
+                nc.sync.dma_start(df0_raw[u][:, slot, :], df0_rows[:, 2 * u + slot, :])
 
         strk_sb = sb("strk_sb", [P, PACK, U], F32, reuse="node_words")
         nc.sync.dma_start(strk_sb[:], strk.rearrange("(p t) r -> p t r", t=PACK))
@@ -154,7 +154,10 @@ def tile_picked_yswapa_val_p_kernel(
         w2_bf = sb("w2_bf", [P, N, PACK], BF16)
         w2_codes = sb("w2_codes", [P, N], U32)
         w2_scales = sb("w2_scales", [P, N], U8)
-        nc.vector.tensor_copy(w2_bf[:], w2_raw[:].rearrange("p j m -> p m j"))
+        nc.vector.tensor_copy(
+            w2_bf[:].rearrange("p (c i) j -> p c j i", i=4),
+            w2_raw[:].rearrange("p j (c i) -> p c j i", i=4),
+        )
         nc.vector.quantize_mx(
             out=w2_codes[:].bitcast(FP8X4),
             scales=w2_scales[:],
@@ -209,6 +212,9 @@ def tile_picked_yswapa_val_p_kernel(
         ann_inv = sb("ann_inv", [P, PACK * V], F32)
         gap = sb("gap", [P, PACK, U], F32)
         sums = {}
+        pieces = [
+            (slice(a, a + PIECE), opt_sb[:, a // 16 : (a + PIECE) // 16]) for a in range(0, U, PIECE)
+        ]
 
         def discount(t):
             u, slot = divmod(t, 2)
@@ -256,9 +262,10 @@ def tile_picked_yswapa_val_p_kernel(
                 )
             for slot in range(2):
                 t = 2 * u + slot
-                nc.vector.tensor_tensor(
-                    gap[:, t, :], swp_win[t][:].indirect(opt_sb[:]), strk_sb[:, t, :], ALU.add
-                )
+                for rs, picks in pieces:
+                    nc.vector.tensor_tensor(
+                        gap[:, t, rs], swp_win[t][:].indirect(picks), strk_sb[:, t, rs], ALU.add
+                    )
 
         for t in range(2):
             discount(t)
@@ -283,14 +290,22 @@ def tile_picked_yswapa_val_p_kernel(
             nc.scalar.activation(sig2[:, t, :], gap[:, t, :], ACT.Sigmoid, scale=4.0)
         weight = sb("weight", [P, PACK, U], F32, reuse="node_words")
         for t in range(SCALAR_GATHERS):
-            nc.scalar.activation(weight[:, t, :], ann_win[t][:].indirect(opt_sb[:]), ACT.Copy)
+            for rs, picks in pieces:
+                nc.scalar.activation(weight[:, t, rs], ann_win[t][:].indirect(picks), ACT.Copy)
+
+        def weave(dst, src):
+            nc.vector.tensor_copy(
+                dst[:].rearrange("p (g i) t -> p g t i", i=4),
+                src[:].rearrange("p t (g i) -> p g t i", i=4),
+            )
 
         weight_il = sb("weight_il", [P, U, PACK], F32, reuse="w1_raw")
         gap_il = sb("gap_il", [P, U, PACK], F32, reuse="scale_rows")
-        nc.vector.tensor_copy(gap_il[:], gap[:].rearrange("p t r -> p r t"))
+        weave(gap_il, gap)
         for t in range(SCALAR_GATHERS, PACK):
-            nc.vector.tensor_copy(weight[:, t, :], ann_win[t][:].indirect(opt_sb[:]))
-        nc.vector.tensor_copy(weight_il[:], weight[:].rearrange("p t r -> p r t"))
+            for rs, picks in pieces:
+                nc.vector.tensor_copy(weight[:, t, rs], ann_win[t][:].indirect(picks))
+        weave(weight_il, weight)
         chunks = U // CHUNK
         logsig2 = [sb(f"logsig2_{c}", [P, CHUNK, PACK], F32, reuse=f"tau{c}") for c in range(chunks)]
         payoff = [sb(f"payoff{c}", [P, CHUNK * PACK], F32, reuse=f"df0_{c}") for c in range(chunks)]
@@ -304,8 +319,8 @@ def tile_picked_yswapa_val_p_kernel(
 
         def take_payoff(c):
             nc.scalar.activation(
-                logsig2[c][:],
-                sig2[:, :, c * CHUNK : (c + 1) * CHUNK].rearrange("p t r -> p r t"),
+                logsig2[c][:].rearrange("p (g i) t -> p g t i", i=4),
+                sig2[:, :, c * CHUNK : (c + 1) * CHUNK].rearrange("p t (g i) -> p g t i", i=4),
                 ACT.Ln,
                 bias=tiny,
             )

from contextlib import ExitStack

import concourse.mybir as mybir
from concourse.masks import make_identity

F32 = mybir.dt.float32
BF16 = mybir.dt.bfloat16
I32 = mybir.dt.int32
U32 = mybir.dt.uint32
U16 = mybir.dt.uint16
U8 = mybir.dt.uint8
FP8X4 = mybir.dt.float8_e4m3fn_x4
ALU = mybir.AluOpType
ACT = mybir.ActivationFunctionType

P = 128
PACK = 4
T, S, H, V, U, N = 2048, 1024, 512, 256, 512, 128
BANK = 512
HALVES = S // BANK
WINDOW = 272
CHUNK = 128
PIECE = 256
SCALAR_GATHERS = 2
D = 4
TINY = 2.0 ** -60

FLOPS = 2 * 512 * 512 * 1024 + 2 * 512 * 128 * 512


def tile_picked_yswapa_val_p_kernel(
    tc, x_words, x_scales, w1, tau, df0, strk, unit, w2, offs, opt, out
):
    nc = tc.nc
    with ExitStack() as ctx:
        keep = ctx.enter_context(tc.tile_pool(name="keep", bufs=1))
        psum = ctx.enter_context(tc.psum_pool(name="psum", bufs=8))

        def sb(name, shape, dtype, reuse=None):
            return keep.tile(shape, dtype, name=name, tag=reuse or name, align_bytes=64)

        offs_sb = keep.tile([P, S // 16], U16, name="offs_sb")
        opt_sb = keep.tile([P, U // 16], U16, name="opt_sb")
        node_words = sb("node_words", [P, T], I32)
        node_scales = sb("node_scales", [P, T], U8)
        scale_rows = sb("scale_rows", [P, T], U8)
        ident = sb("ident", [P, P], F32)
        w1_raw = sb("w1_raw", [P, PACK, H], F32)
        consts = sb("consts", [P, 2], F32)

        nc.vector.memset(node_scales[:].bitcast(I32), 0)
        nc.sync.dma_start(offs_sb[:], offs)
        for q in range(4):
            nc.sync.dma_start(
                scale_rows[32 * q : 32 * q + 4, :].bitcast(I32),
                x_scales[0, 4 * q : 4 * q + 4, :].bitcast(I32),
            )
        nc.sync.dma_start(w1_raw[:], w1.rearrange("(p j) c -> p j c", j=PACK))
        nc.sync.dma_start(node_words[:], x_words[0].rearrange("p n j -> p (n j)").bitcast(I32))
        nc.sync.dma_start(opt_sb[:], opt)
        w2_raw = sb("w2_raw", [P, PACK, N], F32)
        nc.sync.dma_start(w2_raw[:], w2.rearrange("(p j) m -> p j m", j=PACK))
        unit_sb = sb("unit_sb", [P, PACK], F32)
        nc.sync.dma_start(unit_sb[:], unit.rearrange("(p t) o -> p (t o)", t=PACK))

        nc.vector.memset(consts[:, 0:1], TINY)
        nc.vector.memset(consts[:, 1:2], 1.0)
        tiny, one = consts[:, 0:1], consts[:, 1:2]
        ann_win = [sb(f"ann_win{t}", [P, WINDOW], F32) for t in range(PACK)]
        swp_win = [sb(f"swp_win{t}", [P, WINDOW], F32) for t in range(PACK)]
        for win in ann_win + swp_win:
            nc.vector.memset(win[:, V:], 0.0)

        make_identity(nc, ident[:])
        for q in range(4):
            nc.vector.tensor_copy(
                node_scales[32 * q : 32 * q + 4, :].bitcast(I32),
                scale_rows[32 * q : 32 * q + 4, :].bitcast(I32),
            )
        tau_raw = sb("tau_raw", [P, PACK, S], F32, reuse="scale_rows")
        tau_rows = tau.rearrange("(p t) j -> p t j", t=PACK)
        for u in range(2):
            nc.sync.dma_start(tau_raw[:, 2 * u : 2 * u + 2, :], tau_rows[:, 2 * u : 2 * u + 2, :])

        cols = BANK // 16
        picked_scales, picked_words = [], []

        def pick_scales(h, reuse=None):
            picked_scales.append(sb(f"picked_scales{h}", [P, BANK], U8, reuse=reuse))
            nc.vector.tensor_copy(
                picked_scales[h][:], node_scales[:].indirect(offs_sb[:, h * cols : (h + 1) * cols])
            )

        def pick_words(h):
            picked_words.append(sb(f"picked_words{h}", [P, BANK], U32))
            nc.vector.tensor_copy(
                picked_words[h][:],
                node_words[:].bitcast(U32).indirect(offs_sb[:, h * cols : (h + 1) * cols]),
            )

        pick_scales(0)
        w1_bf = sb("w1_bf", [P, PACK * H], BF16)
        w1_codes = sb("w1_codes", [P, H], U32)
        w1_scales = sb("w1_scales", [P, H], U8)
        nc.vector.tensor_copy(
            w1_bf[:].rearrange("p (t m j) -> p m j t", t=PACK, j=PACK),
            w1_raw[:].rearrange("p j (m t) -> p m j t", t=PACK),
        )
        nc.vector.quantize_mx(out=w1_codes[:].bitcast(FP8X4), scales=w1_scales[:], in_=w1_bf[:])
        pick_words(0)
        pick_scales(1, reuse="w1_bf")
        pick_words(1)
        df0_rows = df0.rearrange("(p t) j -> p t j", t=PACK)
        df0_raw = []
        for u, spent in enumerate(("w1_raw", "node_scales")):
            df0_raw.append(sb(f"df0_raw{u}", [P, 2, S], F32, reuse=spent))
            for slot in range(2):
                nc.sync.dma_start(df0_raw[u][:, slot, :], df0_rows[:, 2 * u + slot, :])

        strk_sb = sb("strk_sb", [P, PACK, U], F32, reuse="node_words")
        nc.sync.dma_start(strk_sb[:], strk.rearrange("(p t) r -> p t r", t=PACK))

        def planes(tile, h):
            return tile[:, h * BANK : (h + 1) * BANK].rearrange("p (d v) -> p d v", d=D)

        def by_period(bank):
            return bank[:].rearrange("p (v d) -> p d v", d=D)

        def split_periods(dst, src):
            nc.vector.tensor_copy(
                dst.rearrange("p (h d v) -> p h v d", h=HALVES, d=D),
                src.rearrange("p (h v d) -> p h v d", h=HALVES, d=D),
            )

        fw = {}
        logsig = [sb(f"logsig{t}", [P, S], F32) for t in range(PACK)]
        sig = [sb(f"sig{t}", [P, S], F32) for t in range(PACK)]
        for h in range(HALVES):
            for t in range(PACK):
                fw[t, h] = psum.tile([P, BANK], F32, name="bank")
                nc.tensor.matmul_mx(
                    out=fw[t, h][:],
                    lhsT=w1_codes[:, t * P : (t + 1) * P].bitcast(FP8X4),
                    lhsT_scale=w1_scales[:, t * P : (t + 1) * P],
                    rhs=picked_words[h][:].bitcast(FP8X4),
                    rhs_scale=picked_scales[h][:],
                    start=True,
                    stop=True,
                )
                nc.scalar.activation(
                    planes(sig[t], h), by_period(fw[t, h]), ACT.Sigmoid, scale=-1.0
                )

        w2_bf = sb("w2_bf", [P, N, PACK], BF16)
        w2_codes = sb("w2_codes", [P, N], U32)
        w2_scales = sb("w2_scales", [P, N], U8)
        nc.vector.tensor_copy(
            w2_bf[:].rearrange("p (c i) j -> p c j i", i=4),
            w2_raw[:].rearrange("p j (c i) -> p c j i", i=4),
        )
        nc.vector.quantize_mx(
            out=w2_codes[:].bitcast(FP8X4),
            scales=w2_scales[:],
            in_=w2_bf[:].rearrange("p m j -> p (m j)"),
        )

        unit4 = sb("unit4", [P, PACK], F32)
        nc.vector.tensor_scalar(unit4[:], unit_sb[:], -4.0, None, ALU.mult)

        soft = [sb(f"soft{t}", [P, S], F32) for t in range(PACK)]
        accr = [sb(f"accr{t}", [P, S], F32) for t in range(PACK)]
        tau_sb = [sb(f"tau{t}", [P, S], F32) for t in range(PACK)]
        for t in range(PACK):
            split_periods(tau_sb[t][:], tau_raw[:, t, :])
        for t in range(PACK):
            nc.scalar.activation(logsig[t][:], sig[t][:], ACT.Ln, bias=tiny)
            for h in range(HALVES):
                nc.vector.scalar_tensor_tensor(
                    planes(soft[t], h),
                    planes(logsig[t], h),
                    -1.0,
                    by_period(fw[t, h]),
                    ALU.mult,
                    ALU.max,
                )
            nc.vector.tensor_tensor(accr[t][:], soft[t][:], tau_sb[t][:], ALU.mult)

        def sum_periods(bank, slot, tile):
            for h in range(HALVES):
                block = slot * HALVES + h
                for d in range(D):
                    nc.tensor.matmul(
                        bank[:, block * P : (block + 1) * P],
                        planes(tile, h)[:, d, :],
                        ident[:],
                        start=(d == 0),
                        stop=(d == D - 1),
                        is_transpose=True,
                    )

        def turn_back(name, bank):
            turned = sb(name, [P, BANK], F32)
            nc.scalar.copy(turned[:], bank[:])
            back = psum.tile([P, BANK], F32, name="bank")
            for block in range(BANK // P):
                cs = slice(block * P, (block + 1) * P)
                nc.tensor.transpose(back[:, cs], turned[:, cs], ident[:])
            return back

        df0_sb = [sb(f"df0_{t}", [P, S], F32) for t in range(PACK)]
        ann_root = sb("ann_root", [P, PACK * V], F32)
        ann_inv = sb("ann_inv", [P, PACK * V], F32)
        gap = sb("gap", [P, PACK, U], F32)
        sums = {}
        pieces = [
            (slice(a, a + PIECE), opt_sb[:, a // 16 : (a + PIECE) // 16]) for a in range(0, U, PIECE)
        ]

        def discount(t):
            u, slot = divmod(t, 2)
            if slot == 0:
                sums["ann", u] = psum.tile([P, BANK], F32, name="bank")
                sums["flt", u] = psum.tile([P, BANK], F32, name="bank")
            root, inv, df = sig[t], logsig[t], sig[t]
            split_periods(df0_sb[t][:], df0_raw[u][:, slot, :])
            nc.scalar.activation(root[:], accr[t][:], ACT.Abs_reciprocal_sqrt, bias=one, scale=0.3)
            nc.scalar.activation(inv[:], root[:], ACT.Square)
            nc.vector.tensor_tensor(df[:], inv[:], df0_sb[t][:], ALU.mult)
            sum_periods(sums["ann", u], slot, df)

        def float_leg(t):
            u, slot = divmod(t, 2)
            df, leg = sig[t], accr[t]
            nc.vector.tensor_tensor(leg[:], df[:], soft[t][:], ALU.mult)
            sum_periods(sums["flt", u], slot, leg)

        def invert_annuity(u, ann):
            us = slice(u * BANK, (u + 1) * BANK)
            nc.scalar.activation(ann_root[:, us], ann[:], ACT.Abs_reciprocal_sqrt)
            nc.scalar.activation(ann_inv[:, us], ann_root[:, us], ACT.Square)

        def scale_annuity(u, ann):
            for slot in range(2):
                t = 2 * u + slot
                nc.scalar.activation(
                    ann_win[t][:, :V],
                    ann[:, slot * V : (slot + 1) * V],
                    ACT.Copy,
                    scale=unit4[:, t : t + 1],
                )

        def moneyness(u, flt):
            for slot in range(2):
                t = 2 * u + slot
                nc.vector.scalar_tensor_tensor(
                    swp_win[t][:, :V],
                    flt[:, slot * V : (slot + 1) * V],
                    -0.3,
                    ann_inv[:, t * V : (t + 1) * V],
                    ALU.mult,
                    ALU.mult,
                )
            for slot in range(2):
                t = 2 * u + slot
                for rs, picks in pieces:
                    nc.vector.tensor_tensor(
                        gap[:, t, rs], swp_win[t][:].indirect(picks), strk_sb[:, t, rs], ALU.add
                    )

        for t in range(2):
            discount(t)
            float_leg(t)
        discount(2)
        discount(3)
        ann0 = turn_back("ann_turned0", sums["ann", 0])
        flt0 = turn_back("flt_turned0", sums["flt", 0])
        invert_annuity(0, ann0)
        float_leg(2)
        ann1 = turn_back("ann_turned1", sums["ann", 1])
        float_leg(3)
        flt1 = turn_back("flt_turned1", sums["flt", 1])
        invert_annuity(1, ann1)
        moneyness(0, flt0)
        moneyness(1, flt1)
        scale_annuity(0, ann0)
        scale_annuity(1, ann1)

        sig2 = sb("sig2", [P, PACK, U], F32, reuse="ann_root")
        for t in range(PACK):
            nc.scalar.activation(sig2[:, t, :], gap[:, t, :], ACT.Sigmoid, scale=4.0)
        weight = sb("weight", [P, PACK, U], F32, reuse="node_words")
        for t in range(SCALAR_GATHERS):
            for rs, picks in pieces:
                nc.scalar.activation(weight[:, t, rs], ann_win[t][:].indirect(picks), ACT.Copy)

        def weave(dst, src):
            nc.vector.tensor_copy(
                dst[:].rearrange("p (g i) t -> p g t i", i=4),
                src[:].rearrange("p t (g i) -> p g t i", i=4),
            )

        weight_il = sb("weight_il", [P, U, PACK], F32, reuse="w1_raw")
        gap_il = sb("gap_il", [P, U, PACK], F32, reuse="scale_rows")
        weave(gap_il, gap)
        for t in range(SCALAR_GATHERS, PACK):
            for rs, picks in pieces:
                nc.vector.tensor_copy(weight[:, t, rs], ann_win[t][:].indirect(picks))
        weave(weight_il, weight)
        chunks = U // CHUNK
        logsig2 = [sb(f"logsig2_{c}", [P, CHUNK, PACK], F32, reuse=f"tau{c}") for c in range(chunks)]
        payoff = [sb(f"payoff{c}", [P, CHUNK * PACK], F32, reuse=f"df0_{c}") for c in range(chunks)]
        hid = [sb(f"hid{c}", [P, CHUNK * PACK], BF16) for c in range(chunks)]
        hid_codes = [sb(f"hid_codes{c}", [P, CHUNK], U32) for c in range(chunks)]
        hid_scales = [sb(f"hid_scales{c}", [P, CHUNK], U8) for c in range(chunks)]
        result = [sb(f"result{c}", [P, CHUNK], F32) for c in range(chunks)]

        def rows(tile, c):
            return tile[:, c * CHUNK : (c + 1) * CHUNK, :].rearrange("p r t -> p (r t)")

        def take_payoff(c):
            nc.scalar.activation(
                logsig2[c][:].rearrange("p (g i) t -> p g t i", i=4),
                sig2[:, :, c * CHUNK : (c + 1) * CHUNK].rearrange("p t (g i) -> p g t i", i=4),
                ACT.Ln,
                bias=tiny,
            )
            nc.vector.scalar_tensor_tensor(
                payoff[c][:],
                logsig2[c][:].rearrange("p r t -> p (r t)"),
                0.25,
                rows(gap_il, c),
                ALU.mult,
                ALU.min,
            )

        def weigh(c):
            nc.vector.tensor_tensor(hid[c][:], payoff[c][:], rows(weight_il, c), ALU.mult)

        def book(c):
            nc.vector.quantize_mx(out=hid_codes[c][:].bitcast(FP8X4), scales=hid_scales[c][:], in_=hid[c][:])
            acc = psum.tile([P, BANK], F32, name="bank")
            nc.tensor.matmul_mx(
                out=acc[:, :CHUNK],
                lhsT=w2_codes[:].bitcast(FP8X4),
                lhsT_scale=w2_scales[:],
                rhs=hid_codes[c][:].bitcast(FP8X4),
                rhs_scale=hid_scales[c][:],
                start=True,
                stop=True,
            )
            nc.scalar.copy(result[c][:], acc[:, :CHUNK])
            nc.sync.dma_start(out[:, c * CHUNK : (c + 1) * CHUNK], result[c][:])

        for step in range(chunks + 2):
            if step < chunks:
                take_payoff(step)
            if 1 <= step <= chunks:
                weigh(step - 1)
            if step >= 2:
                book(step - 2)
